import numpy as np, ml_dtypes
CORES = [17,81,89,18,82,90]
N = 6
NH, QP = 12, 32
def setup_inputs(rng):
    return {"q": rng.standard_normal((N, 128, NH * QP), dtype=np.float32).astype(ml_dtypes.bfloat16), "k": rng.standard_normal((N, 128, NH * 128), dtype=np.float32).astype(ml_dtypes.bfloat16), "v": rng.standard_normal((N, 128, NH * 128), dtype=np.float32).astype(ml_dtypes.bfloat16)}
def setup_inputs_big(rng):
    d = setup_inputs(rng)
    for k in ("q", "k", "v"): d[k] = (d[k].astype(np.float32) * 1024.0).astype(d[k].dtype)
    return d
def setup_inputs_small(rng):
    d = setup_inputs(rng)
    for k in ("q", "k", "v"): d[k] = (d[k].astype(np.float32) * (1 / 1024.0)).astype(d[k].dtype)
    return d
def setup_inputs_apart(rng):
    d = setup_inputs(rng)
    f = (10.0 ** rng.permutation(np.linspace(-1.5, 1.5, N))).astype(np.float32).reshape(N, 1, 1)
    for k in ("q", "k", "v"): d[k] = (d[k].astype(np.float32) * f).astype(d[k].dtype)
    return d
def reference(q, k, v):
    Q, K, V = q.astype(np.float64), k.astype(np.float64), v.astype(np.float64)
    y = np.zeros((N, 128, NH * QP))
    for r in range(N):
        for h in range(NH):
            for j in range(N):
                S = np.maximum(K[j][:, 128 * h:128 * h + 128].T @ Q[r][:, QP * h:QP * h + QP], 0.0)
                y[r][:, QP * h:QP * h + QP] += V[j][:, 128 * h:128 * h + 128].T @ S
    return {"y": y.astype(ml_dtypes.bfloat16 if q.dtype != np.float64 else np.float64)}

@@ -1,0 +1,249 @@
+from concourse.bass import DstId, RemoteDMATransfer
+from concourse.mybir import AluOpType
+
+NH, QP = 12, 32
+NG = 2
+HG = NH // NG
+NE = 8
+MAXU = 4
+BF, F32 = "bfloat16", "float32"
+
+SCRATCH = {
+    "qb": ("sbuf", [128, 6, NH, QP], BF),
+    "kb": ("sbuf", [128, NH, 128], BF),
+    "vb": ("sbuf", [128, NH, 128], BF),
+    "zb": ("sbuf", [128, NH, QP], BF),
+    "sb": ("sbuf", [128, MAXU * NG, NH, QP], BF),
+    "pb": ("sbuf", [128, 6, NH, QP], BF),
+    "pl": ("sbuf", [128, 4, NH, QP], BF),
+    "fl": ("sbuf", [128, 3, NH, QP], BF),
+    "yb": ("sbuf", [128, NH, QP], BF),
+}
+for _b in range(8):
+    SCRATCH["ps%d" % _b] = ("psum", [128, 16, QP], F32)
+
+SEMAPHORES = (["qld", "k0", "k1", "v0", "v1", "zs", "sent", "yst", "pa0", "pa1"]
+              + ["qa%d" % r for r in range(6)] + ["fa%d" % i for i in range(3)] + ["fs%d" % i for i in range(3)]
+              + ["%s%d%d" % (c, u, x) for c in "sroc" for u in range(MAXU) for x in range(NG)])
+
+
+def make_plan(cores, topo):
+    n = len(cores)
+    R = range(n)
+    chip = [topo.chip(c) for c in cores]
+    chips = sorted(set(chip))
+    mem = {X: [r for r in R if chip[r] == X] for X in chips}
+    partner = [[p for p in mem[chip[r]] if p != r][0] for r in R]
+    reach = [[X for X in chips if X != chip[r] and all(topo.may_write(cores[r], cores[d]) for d in mem[X])]
+             for r in R]
+    snd = {(H, X): min([r for r in mem[H] if X in reach[r]], key=lambda r: (len(reach[r]), r))
+           for H in chips for X in chips if H != X}
+    load = [len(reach[r]) + 2 * len([X for X in reach[r] if X not in reach[partner[r]]]) for r in R]
+    own_d = [[partner[r]] for r in R]
+    relay_d = [[] for r in R]
+    fwd = [[] for r in R]
+    cls = [[0] * n for r in R]
+    for X in chips:
+        direct = sorted([s for s in R if chip[s] != X and X in reach[s]], key=lambda s: (load[s], s))
+        nboth = max(0, 2 * len(mem[X]) - len(direct))
+        for s in direct[:nboth]:
+            own_d[s] += mem[X]
+            for d in mem[X]:
+                cls[d][s] = 1
+        recv = sorted(mem[X], key=lambda d: (load[d], d))
+        for i, s in enumerate(direct[nboth:][::-1]):
+            d = recv[i % len(recv)]
+            own_d[s].append(d)
+            fwd[d].append(s)
+            cls[d][s], cls[partner[d]][s] = 1, 2
+        for s in R:
+            if chip[s] != X and X not in reach[s]:
+                relay_d[partner[s]] += mem[X]
+                for d in mem[X]:
+                    cls[d][s] = 2
+    for p in R:
+        relay_d[p].sort(key=lambda d: (snd[(chip[d], chip[p])] == d, d))
+
+    def pre(me, r):
+        return snd[(chip[me], chip[r])] != me
+
+    units, slot = [], []
+    for me in R:
+        us = [list(mem[chip[me]])]
+        for c in (1, 2):
+            b = sorted([s for s in R if cls[me][s] == c and chip[s] != chip[me]], key=lambda s: (not pre(me, s), s))
+            if c == 1 or len(set(pre(me, s) for s in b)) == 1:
+                us.append(b)
+            else:
+                us += [[s] for s in b]
+        units.append(us)
+        flat = [s for u in us for s in u]
+        slot.append({s: i for i, s in enumerate(flat)})
+    hand = [[] for r in R]
+    got = [{} for r in R]
+    for me in R:
+        for u in units[me][1:]:
+            pr = [r for r in u if pre(me, r)]
+            if pr:
+                for r in pr:
+                    got[partner[me]][r] = (len(got[partner[me]]), len(hand[me]))
+                hand[me].append(pr)
+    folds = [[] for r in R]
+    fin = [[] for r in R]
+    for me in R:
+        lev = {}
+        for r in R:
+            if chip[r] != chip[me] and not pre(me, r):
+                lev.setdefault(max(cls[me][r], cls[partner[me]][r] + 0.5), []).append(r)
+        for l in sorted(lev):
+            folds[me].append(lev[l])
+            for r in lev[l]:
+                fin[r].append((l, me, len(lev[l])))
+    for r in R:
+        fin[r].sort()
+    return dict(partner=partner, own_d=own_d, relay_d=relay_d, fwd=fwd, units=units, slot=slot, hand=hand, got=got,
+                folds=folds, fin=fin)
+
+
+def rank_program(g, core, T, topo):
+    me = T.rank_of(core)
+    if me is None:
+        return
+    cores = list(T.cores)
+    P = make_plan(cores, topo)
+    sem, te, ve = T.sem, g.tensor, g.vector
+    mate = P["partner"][me]
+    slot, units = P["slot"], P["units"][me]
+
+    m = -1
+    for c in cores:
+        if c != core:
+            m &= topo.mask(core, c)
+    lanes = [b for b in range(m.bit_length()) if (m >> b) & 1][:NE]
+    sent = [0]
+
+    def transfer(srcs, dests, aps, s, part=0, parts=1):
+        w = len(lanes) // parts
+        mask = sum(1 << b for b in lanes[part * w:(part + 1) * w])
+        sent[0] += w
+        ids = [DstId(rid=topo.addr(cores[d])[0], pnc=topo.addr(cores[d])[1]) for d in dests]
+        return RemoteDMATransfer(dst_ids=ids, dma_engine_mask=mask, remote_sem=s, srcs=srcs, dsts=aps,
+                                 alu_op=1 if len(srcs) > 1 else 0)
+
+    def call(transfers):
+        g.remote_dma_fused(transfers, local_sem=sem.sent)
+
+    qs = (g.sync, g.scalar)
+    for i, q in enumerate(qs):
+        q.dma_start(T.qb[64 * i:64 * i + 64, slot[me][me]], T.q[64 * i:64 * i + 64, :]).then_inc(sem.qld, 16)
+    for name, buf, src in (("k", T.kb, T.k), ("v", T.vb, T.v)):
+        for i, q in enumerate(qs):
+            q.dma_start(buf[:, HG * i:HG * i + HG], src[:, 128 * HG * i:128 * HG * (i + 1)]).then_inc(
+                sem["%s%d" % (name, i)], 16)
+    ve.memset(T.zb[:], 0.0).then_inc(sem.zs, 1)
+    ve.wait_ge(sem.zs, 1)
+
+    free = [(b, []) for b in range(8)]
+    acc = []
+    for u, rs in enumerate(units):
+        n = len(rs)
+        s0 = slot[me][rs[0]]
+        for r in rs:
+            if r == me:
+                te.wait_ge(sem.qld, 32)
+            else:
+                te.wait_ge(sem["qa%d" % r], NE)
+        sbank, obank = [], []
+        for x in range(NG):
+            b, conds = free.pop(0)
+            sbank.append(b)
+            for c in conds:
+                te.wait_ge(*c)
+            if u == 0:
+                te.wait_ge(sem["k%d" % x], 16)
+            for hh in range(HG):
+                h = HG * x + hh
+                te.matmul(T["ps%d" % b][:, n * hh:n * hh + n, :], T.kb[:, h, :], T.qb[:, s0:s0 + n, h, :],
+                          True, True).then_inc(sem["s%d%d" % (u, x)], 1)
+        for x in range(NG):
+            ve.wait_ge(sem["s%d%d" % (u, x)], HG)
+            ve.tensor_tensor(T.sb[:, NG * u + x, 0:n * HG, :], T["ps%d" % sbank[x]][:, 0:n * HG, :],
+                             T.zb[:, 0:n * HG, :], AluOpType.max).then_inc(sem["r%d%d" % (u, x)], 1)
+            free.append((sbank[x], [(sem["r%d%d" % (u, x)], 1)]))
+        for x in range(NG):
+            b, conds = free.pop(0)
+            obank.append(b)
+            for c in conds:
+                te.wait_ge(*c)
+            if u == 0:
+                te.wait_ge(sem["v%d" % x], 16)
+            te.wait_ge(sem["r%d%d" % (u, x)], 1)
+            for hh in range(HG):
+                te.matmul(T["ps%d" % b][:, n * hh:n * hh + n, :], T.vb[:, HG * x + hh, :],
+                          T.sb[:, NG * u + x, n * hh:n * hh + n, :], True, True).then_inc(sem["o%d%d" % (u, x)], 1)
+        for x in range(NG):
+            ve.wait_ge(sem["o%d%d" % (u, x)], HG)
+            for i, r in enumerate(rs):
+                view = T["ps%d" % obank[x]][:, i:n * HG:n, :]
+                if r == me:
+                    acc.append(view)
+                else:
+                    ve.tensor_copy(T.pb[:, s0 + i, HG * x:HG * x + HG, :], view).then_inc(sem["c%d%d" % (u, i)], 1)
+        if u > 0:
+            for x in range(NG):
+                free.append((obank[x], [(sem["c%d%d" % (u, i)], NG) for i in range(n)]))
+
+    arrivals = [NE] + [NE // parts for (_, _, parts) in P["fin"][me]]
+    for k, cnt in enumerate(arrivals):
+        ve.wait_ge(sem["fa%d" % k], cnt)
+        if k > 0:
+            ve.wait_ge(sem["fs%d" % (k - 1)], NG)
+        for x in range(NG):
+            out = T.yb[:, HG * x:HG * x + HG, :] if k == len(arrivals) - 1 else acc[x]
+            ve.tensor_tensor(out, acc[x], T.fl[:, k, HG * x:HG * x + HG, :], AluOpType.add).then_inc(
+                sem["fs%d" % k], 1)
+    g.sync.wait_ge(sem["fs%d" % (len(arrivals) - 1)], NG)
+    g.sync.dma_start(T.y[:, :], T.yb[:]).then_inc(sem.yst, 16)
+    g.sync.wait_ge(sem.yst, 16)
+
+    def where(r):
+        for u, rs in enumerate(units):
+            if r in rs:
+                return u, rs.index(r)
+
+    def ready(r):
+        u, i = where(r)
+        g.wait_ge(sem["c%d%d" % (u, i)], NG)
+
+    def send_q(s, dests):
+        call([transfer([T.qb[:, slot[me][s]]], dests, [T.qb[:, slot[d][s]] for d in dests], sem["qa%d" % s])])
+
+    g.wait_ge(sem.qld, 32)
+    send_q(me, P["own_d"][me])
+    if P["relay_d"][me]:
+        g.wait_ge(sem["qa%d" % mate], NE)
+        send_q(mate, P["relay_d"][me])
+    for s in P["fwd"][me]:
+        g.wait_ge(sem["qa%d" % s], NE)
+        send_q(s, [mate])
+    ready(mate)
+    call([transfer([T.pb[:, slot[me][mate]]], [mate], [T.fl[:, 0]], sem.fa0)])
+    for k, rs in enumerate(P["hand"][me]):
+        for r in rs:
+            ready(r)
+        a, b = slot[me][rs[0]], P["got"][mate][rs[0]][0]
+        call([transfer([T.pb[:, a:a + len(rs)]], [mate], [T.pl[:, b:b + len(rs)]], sem["pa%d" % k])])
+    seen = set()
+    for rs in P["folds"][me]:
+        ts = []
+        for j, r in enumerate(rs):
+            ready(r)
+            b, k = P["got"][me][r]
+            if k not in seen:
+                seen.add(k)
+                g.wait_ge(sem["pa%d" % k], NE)
+            idx = 1 + [f[1] for f in P["fin"][r]].index(me)
+            ts.append(transfer([T.pb[:, slot[me][r]], T.pl[:, b]], [r], [T.fl[:, idx]], sem["fa%d" % idx],
+                               j, len(rs)))
+        call(ts)
+    g.wait_ge(sem.sent, sent[0])

@@ -1,141 +1,108 @@
 from concourse.bass import DstId, RemoteDMATransfer
-from concourse.mybir import AluOpType
+from concourse.mybir import AluOpType, ActivationFunctionType
 
 NH, QP = 12, 32
-NG = 2
-HG = NH // NG
+NP = 2
+HG = NH // NP
+NT = 2
+HT = HG // NT
 NE = 8
-MAXU = 4
+WQ = NE // NP
+NSIM = 96
 BF, F32 = "bfloat16", "float32"
 
 SCRATCH = {
-    "qb": ("sbuf", [128, 6, NH, QP], BF),
+    "qb": ("sbuf", [128, 2, NH, QP], BF),
     "kb": ("sbuf", [128, NH, 128], BF),
     "vb": ("sbuf", [128, NH, 128], BF),
     "zb": ("sbuf", [128, NH, QP], BF),
-    "sb": ("sbuf", [128, MAXU * NG, NH, QP], BF),
-    "pb": ("sbuf", [128, 6, NH, QP], BF),
-    "pl": ("sbuf", [128, 4, NH, QP], BF),
+    "sb": ("sbuf", [128, 8, NH, QP], BF),
+    "pl": ("sbuf", [128, NH, QP], BF),
     "fl": ("sbuf", [128, 3, NH, QP], BF),
     "yb": ("sbuf", [128, NH, QP], BF),
+    "hk": ("sbuf", [128, 2, HG, 128], BF),
+    "hv": ("sbuf", [128, 2, HG, 128], BF),
+    "hq": ("sbuf", [128, 4, HG, QP], BF),
+    "rq": ("sbuf", [128, 2, HG, QP], BF),
+    "pb": ("sbuf", [128, 4, HG, QP], BF),
 }
 for _b in range(8):
     SCRATCH["ps%d" % _b] = ("psum", [128, 16, QP], F32)
 
-SEMAPHORES = (["qld", "k0", "k1", "v0", "v1", "zs", "sent", "yst", "pa0", "pa1"]
-              + ["qa%d" % r for r in range(6)] + ["fa%d" % i for i in range(3)] + ["fs%d" % i for i in range(3)]
-              + ["%s%d%d" % (c, u, x) for c in "sroc" for u in range(MAXU) for x in range(NG)])
+SEMAPHORES = (["qld", "k0", "k1", "v0", "v1", "zs", "sent", "yst", "ka0", "ka1", "va0", "va1"]
+              + ["qa%d" % r for r in range(6)] + ["fa%d%d" % (c, i) for c in range(3) for i in range(NP)]
+              + ["fs%d" % i for i in range(3)]
+              + ["%s%d%d" % (c, u, x) for c in "sroc" for u in range(2) for x in range(4)])
 
 
 def make_plan(cores, topo):
-    n = len(cores)
-    R = range(n)
+    R = range(len(cores))
     chip = [topo.chip(c) for c in cores]
     chips = sorted(set(chip))
     mem = {X: [r for r in R if chip[r] == X] for X in chips}
-    partner = [[p for p in mem[chip[r]] if p != r][0] for r in R]
-    reach = [[X for X in chips if X != chip[r] and all(topo.may_write(cores[r], cores[d]) for d in mem[X])]
-             for r in R]
-    snd = {(H, X): min([r for r in mem[H] if X in reach[r]], key=lambda r: (len(reach[r]), r))
-           for H in chips for X in chips if H != X}
-    load = [len(reach[r]) + 2 * len([X for X in reach[r] if X not in reach[partner[r]]]) for r in R]
-    own_d = [[partner[r]] for r in R]
-    relay_d = [[] for r in R]
-    fwd = [[] for r in R]
-    cls = [[0] * n for r in R]
+    helpers, hof = {}, {}
     for X in chips:
-        direct = sorted([s for s in R if chip[s] != X and X in reach[s]], key=lambda s: (load[s], s))
-        nboth = max(0, 2 * len(mem[X]) - len(direct))
-        for s in direct[:nboth]:
-            own_d[s] += mem[X]
-            for d in mem[X]:
-                cls[d][s] = 1
-        recv = sorted(mem[X], key=lambda d: (load[d], d))
-        for i, s in enumerate(direct[nboth:][::-1]):
-            d = recv[i % len(recv)]
-            own_d[s].append(d)
-            fwd[d].append(s)
-            cls[d][s], cls[partner[d]][s] = 1, 2
-        for s in R:
-            if chip[s] != X and X not in reach[s]:
-                relay_d[partner[s]] += mem[X]
-                for d in mem[X]:
-                    cls[d][s] = 2
-    for p in R:
-        relay_d[p].sort(key=lambda d: (snd[(chip[d], chip[p])] == d, d))
-
-    def pre(me, r):
-        return snd[(chip[me], chip[r])] != me
-
-    units, slot = [], []
-    for me in R:
-        us = [list(mem[chip[me]])]
-        for c in (1, 2):
-            b = sorted([s for s in R if cls[me][s] == c and chip[s] != chip[me]], key=lambda s: (not pre(me, s), s))
-            if c == 1 or len(set(pre(me, s) for s in b)) == 1:
-                us.append(b)
-            else:
-                us += [[s] for s in b]
-        units.append(us)
-        flat = [s for u in us for s in u]
-        slot.append({s: i for i, s in enumerate(flat)})
-    hand = [[] for r in R]
-    got = [{} for r in R]
-    for me in R:
-        for u in units[me][1:]:
-            pr = [r for r in u if pre(me, r)]
-            if pr:
-                for r in pr:
-                    got[partner[me]][r] = (len(got[partner[me]]), len(hand[me]))
-                hand[me].append(pr)
-    folds = [[] for r in R]
-    fin = [[] for r in R]
-    for me in R:
-        lev = {}
-        for r in R:
-            if chip[r] != chip[me] and not pre(me, r):
-                lev.setdefault(max(cls[me][r], cls[partner[me]][r] + 0.5), []).append(r)
-        for l in sorted(lev):
-            folds[me].append(lev[l])
-            for r in lev[l]:
-                fin[r].append((l, me, len(lev[l])))
-    for r in R:
-        fin[r].sort()
-    return dict(partner=partner, own_d=own_d, relay_d=relay_d, fwd=fwd, units=units, slot=slot, hand=hand, got=got,
-                folds=folds, fin=fin)
+        el = [c for c in range(NSIM) if topo.chip(c) == X and c not in cores
+              and all(topo.may_write(c, d) for d in cores)]
+        pick = []
+        for c in el:
+            if topo.die(c) not in [topo.die(p) for p in pick]:
+                pick.append(c)
+        pick += [c for c in el if c not in pick]
+        helpers[X] = pick[:NP]
+        for i, c in enumerate(helpers[X]):
+            hof[c] = (X, i)
+    cls = {X: {s: (1 if all(topo.may_write(cores[s], h) for h in helpers[X]) else 2)
+               for s in R if chip[s] != X} for X in chips}
+    units, slot = {}, {}
+    for X in chips:
+        o = sorted(cls[X], key=lambda s: (cls[X][s], s))
+        units[X] = [o[j:j + 2] for j in range(0, len(o), 2)]
+        slot[X] = {s: j for j, s in enumerate(o)}
+    return dict(chip=chip, chips=chips, mem=mem, helpers=helpers, hof=hof, cls=cls, units=units, slot=slot)
 
 
-def rank_program(g, core, T, topo):
-    me = T.rank_of(core)
-    if me is None:
-        return
-    cores = list(T.cores)
-    P = make_plan(cores, topo)
-    sem, te, ve = T.sem, g.tensor, g.vector
-    mate = P["partner"][me]
-    slot, units = P["slot"], P["units"][me]
-
+def lanes_for(topo, core, dests):
     m = -1
-    for c in cores:
-        if c != core:
-            m &= topo.mask(core, c)
-    lanes = [b for b in range(m.bit_length()) if (m >> b) & 1][:NE]
+    for d in dests:
+        m &= topo.mask(core, d)
+    return [b for b in range(m.bit_length()) if (m >> b) & 1]
+
+
+def make_caller(g, T, topo):
     sent = [0]
 
-    def transfer(srcs, dests, aps, s, part=0, parts=1):
-        w = len(lanes) // parts
-        mask = sum(1 << b for b in lanes[part * w:(part + 1) * w])
-        sent[0] += w
-        ids = [DstId(rid=topo.addr(cores[d])[0], pnc=topo.addr(cores[d])[1]) for d in dests]
-        return RemoteDMATransfer(dst_ids=ids, dma_engine_mask=mask, remote_sem=s, srcs=srcs, dsts=aps,
-                                 alu_op=1 if len(srcs) > 1 else 0)
+    def transfer(src, dests, s, lanes):
+        sent[0] += len(lanes)
+        ids = [DstId(rid=topo.addr(c)[0], pnc=topo.addr(c)[1]) for c, _ in dests]
+        return RemoteDMATransfer(dst_ids=ids, dma_engine_mask=sum(1 << b for b in lanes), remote_sem=s,
+                                 srcs=[src], dsts=[ap for _, ap in dests], alu_op=0)
 
-    def call(transfers):
-        g.remote_dma_fused(transfers, local_sem=sem.sent)
+    def call(ts):
+        g.remote_dma_fused(ts, local_sem=T.sem.sent)
+
+    def finish():
+        g.wait_ge(T.sem.sent, sent[0])
+
+    return transfer, call, finish
+
+
+def run_rank(g, core, T, topo, P, me):
+    cores = list(T.cores)
+    sem, te, ve = T.sem, g.tensor, g.vector
+    X = P["chip"][me]
+    chips, helpers, cls, slot = P["chips"], P["helpers"], P["cls"], P["slot"]
+    rs = P["mem"][X]
+    n = len(rs)
+    a = rs.index(me)
+    mate = [r for r in rs if r != me][0]
+    am = rs.index(mate)
+    xi = chips.index(X)
+    transfer, call, finish = make_caller(g, T, topo)
 
     qs = (g.sync, g.scalar)
     for i, q in enumerate(qs):
-        q.dma_start(T.qb[64 * i:64 * i + 64, slot[me][me]], T.q[64 * i:64 * i + 64, :]).then_inc(sem.qld, 16)
+        q.dma_start(T.qb[64 * i:64 * i + 64, a], T.q[64 * i:64 * i + 64, :]).then_inc(sem.qld, 16)
     for name, buf, src in (("k", T.kb, T.k), ("v", T.vb, T.v)):
         for i, q in enumerate(qs):
             q.dma_start(buf[:, HG * i:HG * i + HG], src[:, 128 * HG * i:128 * HG * (i + 1)]).then_inc(
@@ -143,107 +110,166 @@ def rank_program(g, core, T, topo):
     ve.memset(T.zb[:], 0.0).then_inc(sem.zs, 1)
     ve.wait_ge(sem.zs, 1)
 
-    free = [(b, []) for b in range(8)]
-    acc = []
-    for u, rs in enumerate(units):
-        n = len(rs)
-        s0 = slot[me][rs[0]]
-        for r in rs:
-            if r == me:
-                te.wait_ge(sem.qld, 32)
-            else:
-                te.wait_ge(sem["qa%d" % r], NE)
-        sbank, obank = [], []
-        for x in range(NG):
-            b, conds = free.pop(0)
-            sbank.append(b)
-            for c in conds:
-                te.wait_ge(*c)
-            if u == 0:
-                te.wait_ge(sem["k%d" % x], 16)
-            for hh in range(HG):
-                h = HG * x + hh
-                te.matmul(T["ps%d" % b][:, n * hh:n * hh + n, :], T.kb[:, h, :], T.qb[:, s0:s0 + n, h, :],
-                          True, True).then_inc(sem["s%d%d" % (u, x)], 1)
-        for x in range(NG):
-            ve.wait_ge(sem["s%d%d" % (u, x)], HG)
-            ve.tensor_tensor(T.sb[:, NG * u + x, 0:n * HG, :], T["ps%d" % sbank[x]][:, 0:n * HG, :],
-                             T.zb[:, 0:n * HG, :], AluOpType.max).then_inc(sem["r%d%d" % (u, x)], 1)
-            free.append((sbank[x], [(sem["r%d%d" % (u, x)], 1)]))
-        for x in range(NG):
-            b, conds = free.pop(0)
-            obank.append(b)
-            for c in conds:
-                te.wait_ge(*c)
-            if u == 0:
-                te.wait_ge(sem["v%d" % x], 16)
-            te.wait_ge(sem["r%d%d" % (u, x)], 1)
-            for hh in range(HG):
-                te.matmul(T["ps%d" % b][:, n * hh:n * hh + n, :], T.vb[:, HG * x + hh, :],
-                          T.sb[:, NG * u + x, n * hh:n * hh + n, :], True, True).then_inc(sem["o%d%d" % (u, x)], 1)
-        for x in range(NG):
-            ve.wait_ge(sem["o%d%d" % (u, x)], HG)
-            for i, r in enumerate(rs):
-                view = T["ps%d" % obank[x]][:, i:n * HG:n, :]
-                if r == me:
-                    acc.append(view)
-                else:
-                    ve.tensor_copy(T.pb[:, s0 + i, HG * x:HG * x + HG, :], view).then_inc(sem["c%d%d" % (u, i)], 1)
-        if u > 0:
-            for x in range(NG):
-                free.append((obank[x], [(sem["c%d%d" % (u, i)], NG) for i in range(n)]))
+    far = [Y for Y in chips if Y != X and cls[Y][me] == 2]
+    near = [Y for Y in chips if Y != X and cls[Y][me] == 1]
+    alld = [cores[mate]] + [h for Y in chips for h in helpers[Y] if Y not in far]
+    lq = lanes_for(topo, core, alld)[:NE]
+    g.wait_ge(sem.qld, 32)
+    ts = []
+    for i in range(NP):
+        d = []
+        if far:
+            d.append((helpers[X][i], T.rq[:, a]))
+        d += [(helpers[Y][i], T.hq[:, slot[Y][me]]) for Y in near]
+        d.append((cores[mate], T.qb[:, a, HG * i:HG * i + HG, :]))
+        ts.append(transfer(T.qb[:, a, HG * i:HG * i + HG, :], d, sem["qa%d" % me], lq[WQ * i:WQ * i + WQ]))
+    call(ts)
+    lk = lanes_for(topo, core, helpers[X])
+    wk = len(lk) // NP
+    for name, buf, dst in (("k", T.kb, T.hk), ("v", T.vb, T.hv)):
+        for i in range(NP):
+            g.wait_ge(sem["%s%d" % (name, i)], 16)
+        call([transfer(buf[:, HG * i:HG * i + HG, :], [(helpers[X][i], dst[:, a])], sem["%sa%d" % (name, a)],
+                       lk[wk * i:wk * i + wk]) for i in range(NP)])
+    g.wait_ge(sem.c00, NP)
+    call([transfer(T.pl[:], [(cores[mate], T.fl[:, xi])], sem["fa%d0" % xi], lq)])
+    finish()
 
-    arrivals = [NE] + [NE // parts for (_, _, parts) in P["fin"][me]]
-    for k, cnt in enumerate(arrivals):
-        ve.wait_ge(sem["fa%d" % k], cnt)
+    te.wait_ge(sem.qld, 32)
+    te.wait_ge(sem["qa%d" % mate], NE)
+    for x in range(NP):
+        te.wait_ge(sem["k%d" % x], 16)
+        for hh in range(HG):
+            te.matmul(T["ps%d" % x][:, n * hh:n * hh + n, :], T.kb[:, HG * x + hh, :], T.qb[:, 0:n, HG * x + hh, :],
+                      True, True).then_inc(sem["s0%d" % x], 1)
+    for x in range(NP):
+        ve.wait_ge(sem["s0%d" % x], HG)
+        ve.tensor_tensor(T.sb[:, x, 0:n * HG, :], T["ps%d" % x][:, 0:n * HG, :], T.zb[:, 0:n * HG, :],
+                         AluOpType.max).then_inc(sem["r0%d" % x], 1)
+    for x in range(NP):
+        te.wait_ge(sem["v%d" % x], 16)
+        te.wait_ge(sem["r0%d" % x], 1)
+        for hh in range(HG):
+            te.matmul(T["ps%d" % (NP + x)][:, n * hh:n * hh + n, :], T.vb[:, HG * x + hh, :],
+                      T.sb[:, x, n * hh:n * hh + n, :], True, True).then_inc(sem["o0%d" % x], 1)
+    acc = []
+    for x in range(NP):
+        ve.wait_ge(sem["o0%d" % x], HG)
+        ve.tensor_copy(T.pl[:, HG * x:HG * x + HG, :], T["ps%d" % (NP + x)][:, am:n * HG:n, :]).then_inc(sem.c00, 1)
+        acc.append(T["ps%d" % (NP + x)][:, a:n * HG:n, :])
+
+    def when(Y):
+        return [u for u, q in enumerate(P["units"][Y]) if me in q][0]
+
+    order = [X] + sorted([Y for Y in chips if Y != X], key=lambda Y: (when(Y), cls[Y][me], Y))
+    for k, Y in enumerate(order):
+        yi = chips.index(Y)
         if k > 0:
-            ve.wait_ge(sem["fs%d" % (k - 1)], NG)
-        for x in range(NG):
-            out = T.yb[:, HG * x:HG * x + HG, :] if k == len(arrivals) - 1 else acc[x]
-            ve.tensor_tensor(out, acc[x], T.fl[:, k, HG * x:HG * x + HG, :], AluOpType.add).then_inc(
+            ve.wait_ge(sem["fs%d" % (k - 1)], NP)
+        for x in range(NP):
+            if Y == X:
+                ve.wait_ge(sem["fa%d0" % yi], NE)
+            else:
+                ve.wait_ge(sem["fa%d%d" % (yi, x)], WQ)
+            out = T.yb[:, HG * x:HG * x + HG, :] if k == len(order) - 1 else acc[x]
+            ve.tensor_tensor(out, acc[x], T.fl[:, yi, HG * x:HG * x + HG, :], AluOpType.add).then_inc(
                 sem["fs%d" % k], 1)
-    g.sync.wait_ge(sem["fs%d" % (len(arrivals) - 1)], NG)
+    g.sync.wait_ge(sem["fs%d" % (len(order) - 1)], NP)
     g.sync.dma_start(T.y[:, :], T.yb[:]).then_inc(sem.yst, 16)
     g.sync.wait_ge(sem.yst, 16)
 
-    def where(r):
-        for u, rs in enumerate(units):
-            if r in rs:
-                return u, rs.index(r)
 
-    def ready(r):
-        u, i = where(r)
-        g.wait_ge(sem["c%d%d" % (u, i)], NG)
+def run_helper(g, core, T, topo, P, X, i):
+    cores = list(T.cores)
+    sem, te, ve, sc = T.sem, g.tensor, g.vector, g.scalar
+    chips, helpers, cls, slot, units = P["chips"], P["helpers"], P["cls"], P["slot"][X], P["units"][X]
+    xi = chips.index(X)
+    transfer, call, finish = make_caller(g, T, topo)
+    lanes = lanes_for(topo, core, cores + [h for Y in chips for h in helpers[Y] if h != core])[:NE]
+    wk = len(lanes_for(topo, cores[P["mem"][X][0]], helpers[X])) // NP
+    NX = NT * 2
 
-    def send_q(s, dests):
-        call([transfer([T.qb[:, slot[me][s]]], dests, [T.qb[:, slot[d][s]] for d in dests], sem["qa%d" % s])])
+    ve.memset(T.zb[:], 0.0).then_inc(sem.zs, 1)
+    ve.wait_ge(sem.zs, 1)
 
-    g.wait_ge(sem.qld, 32)
-    send_q(me, P["own_d"][me])
-    if P["relay_d"][me]:
-        g.wait_ge(sem["qa%d" % mate], NE)
-        send_q(mate, P["relay_d"][me])
-    for s in P["fwd"][me]:
-        g.wait_ge(sem["qa%d" % s], NE)
-        send_q(s, [mate])
-    ready(mate)
-    call([transfer([T.pb[:, slot[me][mate]]], [mate], [T.fl[:, 0]], sem.fa0)])
-    for k, rs in enumerate(P["hand"][me]):
-        for r in rs:
-            ready(r)
-        a, b = slot[me][rs[0]], P["got"][mate][rs[0]][0]
-        call([transfer([T.pb[:, a:a + len(rs)]], [mate], [T.pl[:, b:b + len(rs)]], sem["pa%d" % k])])
-    seen = set()
-    for rs in P["folds"][me]:
+    for a, s in enumerate(P["mem"][X]):
+        far = [Y for Y in chips if Y != X and cls[Y][s] == 2]
+        if far:
+            g.wait_ge(sem["qa%d" % s], WQ)
+            call([transfer(T.rq[:, a], [(helpers[Y][i], T.hq[:, P["slot"][Y][s]]) for Y in far],
+                           sem["qa%d" % s], lanes)])
+    for u, rs in enumerate(units):
+        w = NE // len(rs)
         ts = []
         for j, r in enumerate(rs):
-            ready(r)
-            b, k = P["got"][me][r]
-            if k not in seen:
-                seen.add(k)
-                g.wait_ge(sem["pa%d" % k], NE)
-            idx = 1 + [f[1] for f in P["fin"][r]].index(me)
-            ts.append(transfer([T.pb[:, slot[me][r]], T.pl[:, b]], [r], [T.fl[:, idx]], sem["fa%d" % idx],
-                               j, len(rs)))
+            g.wait_ge(sem["c%d%d" % (u, j)], NT)
+            ts.append(transfer(T.pb[:, slot[r]], [(cores[r], T.fl[:, xi, HG * i:HG * i + HG, :])],
+                               sem["fa%d%d" % (xi, i)], lanes[w * j:w * j + w]))
         call(ts)
-    g.wait_ge(sem.sent, sent[0])
+    finish()
+
+    free = [(b, []) for b in range(8)]
+
+    def bank():
+        b, conds = free.pop(0)
+        for c in conds:
+            te.wait_ge(*c)
+        return b
+
+    for u, rs in enumerate(units):
+        n, s0 = len(rs), slot[rs[0]]
+        for r in rs:
+            te.wait_ge(sem["qa%d" % r], WQ if cls[X][r] == 1 else NE)
+        for x in range(NX):
+            t, a = divmod(x, 2)
+            b = bank()
+            if u == 0 and t == 0:
+                te.wait_ge(sem["ka%d" % a], wk)
+            for hh in range(HT):
+                te.matmul(T["ps%d" % b][:, n * hh:n * hh + n, :], T.hk[:, a, HT * t + hh, :],
+                          T.hq[:, s0:s0 + n, HT * t + hh, :], True, True).then_inc(sem["s%d%d" % (u, x)], 1)
+            e = ve if a == 0 else sc
+            e.wait_ge(sem["s%d%d" % (u, x)], HT)
+            if a == 0:
+                ins = ve.tensor_tensor(T.sb[:, NX * u + x, 0:n * HT, :], T["ps%d" % b][:, 0:n * HT, :],
+                                       T.zb[:, 0:n * HT, :], AluOpType.max)
+            else:
+                ins = sc.activation(T.sb[:, NX * u + x, 0:n * HT, :], T["ps%d" % b][:, 0:n * HT, :],
+                                    ActivationFunctionType.Relu)
+            ins.then_inc(sem["r%d%d" % (u, x)], 1)
+            free.append((b, [(sem["r%d%d" % (u, x)], 1)]))
+    for u, rs in enumerate(units):
+        n, s0 = len(rs), slot[rs[0]]
+        for t in range(NT):
+            b = bank()
+            if u == 0 and t == 0:
+                for a in range(2):
+                    te.wait_ge(sem["va%d" % a], wk)
+            for a in range(2):
+                te.wait_ge(sem["r%d%d" % (u, 2 * t + a)], 1)
+            for hh in range(HT):
+                for a in range(2):
+                    te.matmul(T["ps%d" % b][:, n * hh:n * hh + n, :], T.hv[:, a, HT * t + hh, :],
+                              T.sb[:, NX * u + 2 * t + a, n * hh:n * hh + n, :], a == 0, a == 1).then_inc(
+                        sem["o%d%d" % (u, t)], 1)
+            e = ve if t == 0 else sc
+            e.wait_ge(sem["o%d%d" % (u, t)], 2 * HT)
+            for j in range(n):
+                view = T["ps%d" % b][:, j:n * HT:n, :]
+                out = T.pb[:, s0 + j, HT * t:HT * t + HT, :]
+                if t == 0:
+                    ins = ve.tensor_copy(out, view)
+                else:
+                    ins = sc.activation(out, view, ActivationFunctionType.Copy)
+                ins.then_inc(sem["c%d%d" % (u, j)], 1)
+            free.append((b, [(sem["c%d%d" % (u, j)], NT) for j in range(n)]))
+
+
+def rank_program(g, core, T, topo):
+    P = make_plan(list(T.cores), topo)
+    me = T.rank_of(core)
+    if me is not None:
+        run_rank(g, core, T, topo, P, me)
+    elif core in P["hof"]:
+        X, i = P["hof"][core]
+        run_helper(g, core, T, topo, P, X, i)

from concourse.bass import DstId, RemoteDMATransfer
from concourse.mybir import AluOpType, ActivationFunctionType

NH, QP = 12, 32
NP = 2
HG = NH // NP
NT = 2
HT = HG // NT
NE = 8
WQ = NE // NP
NSIM = 96
BF, F32 = "bfloat16", "float32"

SCRATCH = {
    "qb": ("sbuf", [128, 2, NH, QP], BF),
    "kb": ("sbuf", [128, NH, 128], BF),
    "vb": ("sbuf", [128, NH, 128], BF),
    "zb": ("sbuf", [128, NH, QP], BF),
    "sb": ("sbuf", [128, 8, NH, QP], BF),
    "pl": ("sbuf", [128, NH, QP], BF),
    "fl": ("sbuf", [128, 3, NH, QP], BF),
    "yb": ("sbuf", [128, NH, QP], BF),
    "hk": ("sbuf", [128, 2, HG, 128], BF),
    "hv": ("sbuf", [128, 2, HG, 128], BF),
    "hq": ("sbuf", [128, 4, HG, QP], BF),
    "rq": ("sbuf", [128, 2, HG, QP], BF),
    "pb": ("sbuf", [128, 4, HG, QP], BF),
}
for _b in range(8):
    SCRATCH["ps%d" % _b] = ("psum", [128, 16, QP], F32)

SEMAPHORES = (["qld", "k0", "k1", "v0", "v1", "zs", "sent", "yst", "ka0", "ka1", "va0", "va1"]
              + ["qa%d" % r for r in range(6)] + ["fa%d%d" % (c, i) for c in range(3) for i in range(NP)]
              + ["fs%d" % i for i in range(3)]
              + ["%s%d%d" % (c, u, x) for c in "sroc" for u in range(2) for x in range(4)])


def make_plan(cores, topo):
    R = range(len(cores))
    chip = [topo.chip(c) for c in cores]
    chips = sorted(set(chip))
    mem = {X: [r for r in R if chip[r] == X] for X in chips}
    helpers, hof = {}, {}
    for X in chips:
        el = [c for c in range(NSIM) if topo.chip(c) == X and c not in cores
              and all(topo.may_write(c, d) for d in cores)]
        pick = []
        for c in el:
            if topo.die(c) not in [topo.die(p) for p in pick]:
                pick.append(c)
        pick += [c for c in el if c not in pick]
        helpers[X] = pick[:NP]
        for i, c in enumerate(helpers[X]):
            hof[c] = (X, i)
    cls = {X: {s: (1 if all(topo.may_write(cores[s], h) for h in helpers[X]) else 2)
               for s in R if chip[s] != X} for X in chips}
    units, slot = {}, {}
    for X in chips:
        o = sorted(cls[X], key=lambda s: (cls[X][s], s))
        units[X] = [o[j:j + 2] for j in range(0, len(o), 2)]
        slot[X] = {s: j for j, s in enumerate(o)}
    return dict(chip=chip, chips=chips, mem=mem, helpers=helpers, hof=hof, cls=cls, units=units, slot=slot)


def lanes_for(topo, core, dests):
    m = -1
    for d in dests:
        m &= topo.mask(core, d)
    return [b for b in range(m.bit_length()) if (m >> b) & 1]


def make_caller(g, T, topo):
    sent = [0]

    def transfer(src, dests, s, lanes):
        sent[0] += len(lanes)
        ids = [DstId(rid=topo.addr(c)[0], pnc=topo.addr(c)[1]) for c, _ in dests]
        return RemoteDMATransfer(dst_ids=ids, dma_engine_mask=sum(1 << b for b in lanes), remote_sem=s,
                                 srcs=[src], dsts=[ap for _, ap in dests], alu_op=0)

    def call(ts):
        g.remote_dma_fused(ts, local_sem=T.sem.sent)

    def finish():
        g.wait_ge(T.sem.sent, sent[0])

    return transfer, call, finish


def run_rank(g, core, T, topo, P, me):
    cores = list(T.cores)
    sem, te, ve = T.sem, g.tensor, g.vector
    X = P["chip"][me]
    chips, helpers, cls, slot = P["chips"], P["helpers"], P["cls"], P["slot"]
    rs = P["mem"][X]
    n = len(rs)
    a = rs.index(me)
    mate = [r for r in rs if r != me][0]
    am = rs.index(mate)
    xi = chips.index(X)
    transfer, call, finish = make_caller(g, T, topo)

    qs = (g.sync, g.scalar)
    for i, q in enumerate(qs):
        q.dma_start(T.qb[64 * i:64 * i + 64, a], T.q[64 * i:64 * i + 64, :]).then_inc(sem.qld, 16)
    for name, buf, src in (("k", T.kb, T.k), ("v", T.vb, T.v)):
        for i, q in enumerate(qs):
            q.dma_start(buf[:, HG * i:HG * i + HG], src[:, 128 * HG * i:128 * HG * (i + 1)]).then_inc(
                sem["%s%d" % (name, i)], 16)
    ve.memset(T.zb[:], 0.0).then_inc(sem.zs, 1)
    ve.wait_ge(sem.zs, 1)

    far = [Y for Y in chips if Y != X and cls[Y][me] == 2]
    near = [Y for Y in chips if Y != X and cls[Y][me] == 1]
    alld = [cores[mate]] + [h for Y in chips for h in helpers[Y] if Y not in far]
    lq = lanes_for(topo, core, alld)[:NE]
    g.wait_ge(sem.qld, 32)
    ts = []
    for i in range(NP):
        d = []
        if far:
            d.append((helpers[X][i], T.rq[:, a]))
        d += [(helpers[Y][i], T.hq[:, slot[Y][me]]) for Y in near]
        d.append((cores[mate], T.qb[:, a, HG * i:HG * i + HG, :]))
        ts.append(transfer(T.qb[:, a, HG * i:HG * i + HG, :], d, sem["qa%d" % me], lq[WQ * i:WQ * i + WQ]))
    call(ts)
    lk = lanes_for(topo, core, helpers[X])
    wk = len(lk) // NP
    for name, buf, dst in (("k", T.kb, T.hk), ("v", T.vb, T.hv)):
        for i in range(NP):
            g.wait_ge(sem["%s%d" % (name, i)], 16)
        call([transfer(buf[:, HG * i:HG * i + HG, :], [(helpers[X][i], dst[:, a])], sem["%sa%d" % (name, a)],
                       lk[wk * i:wk * i + wk]) for i in range(NP)])
    g.wait_ge(sem.c00, NP)
    call([transfer(T.pl[:], [(cores[mate], T.fl[:, xi])], sem["fa%d0" % xi], lq)])
    finish()

    te.wait_ge(sem.qld, 32)
    te.wait_ge(sem["qa%d" % mate], NE)
    for x in range(NP):
        te.wait_ge(sem["k%d" % x], 16)
        for hh in range(HG):
            te.matmul(T["ps%d" % x][:, n * hh:n * hh + n, :], T.kb[:, HG * x + hh, :], T.qb[:, 0:n, HG * x + hh, :],
                      True, True).then_inc(sem["s0%d" % x], 1)
    for x in range(NP):
        ve.wait_ge(sem["s0%d" % x], HG)
        ve.tensor_tensor(T.sb[:, x, 0:n * HG, :], T["ps%d" % x][:, 0:n * HG, :], T.zb[:, 0:n * HG, :],
                         AluOpType.max).then_inc(sem["r0%d" % x], 1)
    for x in range(NP):
        te.wait_ge(sem["v%d" % x], 16)
        te.wait_ge(sem["r0%d" % x], 1)
        for hh in range(HG):
            te.matmul(T["ps%d" % (NP + x)][:, n * hh:n * hh + n, :], T.vb[:, HG * x + hh, :],
                      T.sb[:, x, n * hh:n * hh + n, :], True, True).then_inc(sem["o0%d" % x], 1)
    acc = []
    for x in range(NP):
        ve.wait_ge(sem["o0%d" % x], HG)
        ve.tensor_copy(T.pl[:, HG * x:HG * x + HG, :], T["ps%d" % (NP + x)][:, am:n * HG:n, :]).then_inc(sem.c00, 1)
        acc.append(T["ps%d" % (NP + x)][:, a:n * HG:n, :])

    def when(Y):
        return [u for u, q in enumerate(P["units"][Y]) if me in q][0]

    order = [X] + sorted([Y for Y in chips if Y != X], key=lambda Y: (when(Y), cls[Y][me], Y))
    for k, Y in enumerate(order):
        yi = chips.index(Y)
        if k > 0:
            ve.wait_ge(sem["fs%d" % (k - 1)], NP)
        for x in range(NP):
            if Y == X:
                ve.wait_ge(sem["fa%d0" % yi], NE)
            else:
                ve.wait_ge(sem["fa%d%d" % (yi, x)], WQ)
            out = T.yb[:, HG * x:HG * x + HG, :] if k == len(order) - 1 else acc[x]
            ve.tensor_tensor(out, acc[x], T.fl[:, yi, HG * x:HG * x + HG, :], AluOpType.add).then_inc(
                sem["fs%d" % k], 1)
    g.sync.wait_ge(sem["fs%d" % (len(order) - 1)], NP)
    g.sync.dma_start(T.y[:, :], T.yb[:]).then_inc(sem.yst, 16)
    g.sync.wait_ge(sem.yst, 16)


def run_helper(g, core, T, topo, P, X, i):
    cores = list(T.cores)
    sem, te, ve, sc = T.sem, g.tensor, g.vector, g.scalar
    chips, helpers, cls, slot, units = P["chips"], P["helpers"], P["cls"], P["slot"][X], P["units"][X]
    xi = chips.index(X)
    transfer, call, finish = make_caller(g, T, topo)
    lanes = lanes_for(topo, core, cores + [h for Y in chips for h in helpers[Y] if h != core])[:NE]
    wk = len(lanes_for(topo, cores[P["mem"][X][0]], helpers[X])) // NP
    NX = NT * 2

    ve.memset(T.zb[:], 0.0).then_inc(sem.zs, 1)
    ve.wait_ge(sem.zs, 1)

    for a, s in enumerate(P["mem"][X]):
        far = [Y for Y in chips if Y != X and cls[Y][s] == 2]
        if far:
            g.wait_ge(sem["qa%d" % s], WQ)
            call([transfer(T.rq[:, a], [(helpers[Y][i], T.hq[:, P["slot"][Y][s]]) for Y in far],
                           sem["qa%d" % s], lanes)])
    for u, rs in enumerate(units):
        w = NE // len(rs)
        ts = []
        for j, r in enumerate(rs):
            g.wait_ge(sem["c%d%d" % (u, j)], NT)
            ts.append(transfer(T.pb[:, slot[r]], [(cores[r], T.fl[:, xi, HG * i:HG * i + HG, :])],
                               sem["fa%d%d" % (xi, i)], lanes[w * j:w * j + w]))
        call(ts)
    finish()

    free = [(b, []) for b in range(8)]

    def bank():
        b, conds = free.pop(0)
        for c in conds:
            te.wait_ge(*c)
        return b

    for u, rs in enumerate(units):
        n, s0 = len(rs), slot[rs[0]]
        for r in rs:
            te.wait_ge(sem["qa%d" % r], WQ if cls[X][r] == 1 else NE)
        for x in range(NX):
            t, a = divmod(x, 2)
            b = bank()
            if u == 0 and t == 0:
                te.wait_ge(sem["ka%d" % a], wk)
            for hh in range(HT):
                te.matmul(T["ps%d" % b][:, n * hh:n * hh + n, :], T.hk[:, a, HT * t + hh, :],
                          T.hq[:, s0:s0 + n, HT * t + hh, :], True, True).then_inc(sem["s%d%d" % (u, x)], 1)
            e = ve if a == 0 else sc
            e.wait_ge(sem["s%d%d" % (u, x)], HT)
            if a == 0:
                ins = ve.tensor_tensor(T.sb[:, NX * u + x, 0:n * HT, :], T["ps%d" % b][:, 0:n * HT, :],
                                       T.zb[:, 0:n * HT, :], AluOpType.max)
            else:
                ins = sc.activation(T.sb[:, NX * u + x, 0:n * HT, :], T["ps%d" % b][:, 0:n * HT, :],
                                    ActivationFunctionType.Relu)
            ins.then_inc(sem["r%d%d" % (u, x)], 1)
            free.append((b, [(sem["r%d%d" % (u, x)], 1)]))
    for u, rs in enumerate(units):
        n, s0 = len(rs), slot[rs[0]]
        for t in range(NT):
            b = bank()
            if u == 0 and t == 0:
                for a in range(2):
                    te.wait_ge(sem["va%d" % a], wk)
            for a in range(2):
                te.wait_ge(sem["r%d%d" % (u, 2 * t + a)], 1)
            for hh in range(HT):
                for a in range(2):
                    te.matmul(T["ps%d" % b][:, n * hh:n * hh + n, :], T.hv[:, a, HT * t + hh, :],
                              T.sb[:, NX * u + 2 * t + a, n * hh:n * hh + n, :], a == 0, a == 1).then_inc(
                        sem["o%d%d" % (u, t)], 1)
            e = ve if t == 0 else sc
            e.wait_ge(sem["o%d%d" % (u, t)], 2 * HT)
            for j in range(n):
                view = T["ps%d" % b][:, j:n * HT:n, :]
                out = T.pb[:, s0 + j, HT * t:HT * t + HT, :]
                if t == 0:
                    ins = ve.tensor_copy(out, view)
                else:
                    ins = sc.activation(out, view, ActivationFunctionType.Copy)
                ins.then_inc(sem["c%d%d" % (u, j)], 1)
            free.append((b, [(sem["c%d%d" % (u, j)], NT) for j in range(n)]))


def rank_program(g, core, T, topo):
    P = make_plan(list(T.cores), topo)
    me = T.rank_of(core)
    if me is not None:
        run_rank(g, core, T, topo, P, me)
    elif core in P["hof"]:
        X, i = P["hof"][core]
        run_helper(g, core, T, topo, P, X, i)
